import numpy as np, ml_dtypes
CORES = [51,54,179,182]
N = 4
TK = 32
def setup_inputs(rng):
    return {"x": rng.standard_normal((N, 128, N * TK), dtype=np.float32).astype(ml_dtypes.bfloat16), "t": rng.standard_normal((N, 128, N * TK), dtype=np.float32).astype(ml_dtypes.bfloat16), "f1": (rng.standard_normal((N, 128, 128), dtype=np.float32) / 11).astype(ml_dtypes.bfloat16), "f2": (rng.standard_normal((N, 128, 128), dtype=np.float32) / 11).astype(ml_dtypes.bfloat16)}
def setup_inputs_big(rng):
    d = setup_inputs(rng)
    for k in ("x", "t", "f1", "f2"): d[k] = (d[k].astype(np.float32) * 1024.0).astype(d[k].dtype)
    return d
def setup_inputs_small(rng):
    d = setup_inputs(rng)
    for k in ("x", "t", "f1", "f2"): d[k] = (d[k].astype(np.float32) * (1 / 1024.0)).astype(d[k].dtype)
    return d
def setup_inputs_apart(rng):
    d = setup_inputs(rng)
    f = (10.0 ** rng.permutation(np.linspace(-1.5, 1.5, N))).astype(np.float32).reshape(N, 1, 1)
    for k in ("x", "t", "f1", "f2"): d[k] = (d[k].astype(np.float32) * f).astype(d[k].dtype)
    return d
def reference(x, t, f1, f2):
    X, T, F1, F2 = x.astype(np.float64), t.astype(np.float64), f1.astype(np.float64), f2.astype(np.float64)
    y = np.zeros((N, 128, N * TK))
    for j in range(N):
        u = (F1[j].T @ X[j]) * T[j]
        for r in range(N):
            y[r][:, TK * j:TK * j + TK] = F2[r].T @ u[:, TK * r:TK * r + TK]
    return {"y": y.astype(ml_dtypes.bfloat16)}

@@ -1,0 +1,123 @@
+from concourse.bass import DstId, RemoteDMATransfer
+from concourse.mybir import AluOpType
+
+P, TK, N = 128, 32, 4
+W = N * TK
+K_FAR = 4
+K_NEAR = 4
+
+SCRATCH = {
+    "xs": ("sbuf", [P, W], "bfloat16"),
+    "ts": ("sbuf", [P, W], "bfloat16"),
+    "f1s": ("sbuf", [P, P], "bfloat16"),
+    "f2s": ("sbuf", [P, P], "bfloat16"),
+    "us": ("sbuf", [P, W], "bfloat16"),
+    "land": ("sbuf", [P, W], "bfloat16"),
+    "ys": ("sbuf", [P, W], "bfloat16"),
+    "pu": ("psum", [P, 512], "float32"),
+    "pn": ("psum", [P, 512], "float32"),
+    "pf": ("psum", [P, 512], "float32"),
+}
+SEMAPHORES = ["ld_mm", "ld_t", "ld_f2", "mm_u", "u_ok", "sent", "arr_near", "arr_far",
+              "mm_near", "mm_far", "cp_near", "cp_far", "stored"]
+
+
+def _blk(j):
+    return slice(TK * j, TK * j + TK)
+
+
+def _runs(js):
+    out = []
+    for j in sorted(js):
+        if out and out[-1][1] == j:
+            out[-1][1] = j + 1
+        else:
+            out.append([j, j + 1])
+    return [slice(TK * a, TK * b) for a, b in out]
+
+
+def _engines(m):
+    return [e for e in range(m.bit_length()) if (m >> e) & 1]
+
+
+def _to_mask(es):
+    m = 0
+    for e in es:
+        m |= 1 << e
+    return m
+
+
+def rank_program(g, core, T, topo):
+    r = T.rank_of(core)
+    if r is None:
+        return
+    S = T.sem
+    here = (topo.host(core), topo.chip(core))
+    near = [j for j, c in enumerate(T.cores) if (topo.host(c), topo.chip(c)) == here]
+    far = [j for j in range(len(T.cores)) if j not in near]
+    near_peers = [j for j in near if j != r]
+
+    g.sync.dma_start(T.xs[:], T.x[:]).then_inc(S.ld_mm, 16)
+    g.scalar.dma_start(T.f1s[:], T.f1[:]).then_inc(S.ld_mm, 16)
+    g.sync.dma_start(T.ts[:], T.t[:]).then_inc(S.ld_t, 16)
+    g.sync.dma_start(T.f2s[:], T.f2[:]).then_inc(S.ld_f2, 16)
+
+    g.tensor.wait_ge(S.ld_mm, 32)
+    g.tensor.matmul(T.pu[:, 0:W], T.f1s[:], T.xs[:], True, True).then_inc(S.mm_u, 1)
+    g.vector.wait_ge(S.ld_t, 16)
+    g.vector.wait_ge(S.mm_u, 1)
+    g.vector.tensor_tensor(T.us[:], T.pu[:, 0:W], T.ts[:], AluOpType.mult).then_inc(S.u_ok, 1)
+
+    used = []
+    plan = []
+    for j in far:
+        free = [e for e in _engines(topo.mask(core, T.cores[j])) if e not in used]
+        plan.append((j, free[:K_FAR], S.arr_far))
+        used += free[:K_FAR]
+    off_chip = []
+    for j in far:
+        off_chip += _engines(topo.mask(core, T.cores[j]))
+    for j in near_peers:
+        free = [e for e in _engines(topo.mask(core, T.cores[j])) if e not in used]
+        pref = [e for e in free if e not in off_chip] or free
+        share = len(pref) // len(near_peers)
+        pick = pref[::max(1, share // K_NEAR)][:K_NEAR]
+        plan.append((j, pick, S.arr_near))
+        used += pick
+    transfers = []
+    for j, es, sem in plan:
+        rid, pid = topo.addr(T.cores[j], core)
+        transfers.append(RemoteDMATransfer(dst_ids=[DstId(rid=rid, pnc=pid)], dma_engine_mask=_to_mask(es),
+                                           remote_sem=sem, src=T.us[:, _blk(j)], dst=T.land[:, _blk(r)]))
+    g.wait_ge(S.u_ok, 1)
+    g.remote_dma_fused(transfers, local_sem=S.sent)
+
+    g.tensor.wait_ge(S.ld_f2, 16)
+    g.tensor.wait_ge(S.u_ok, 1)
+    g.tensor.matmul(T.pn[:, _blk(r)], T.f2s[:], T.us[:, _blk(r)], True, True).then_inc(S.mm_near, 1)
+    n_mm = 1
+    if near_peers:
+        g.tensor.wait_ge(S.arr_near, K_NEAR * len(near_peers))
+        for run in _runs(near_peers):
+            g.tensor.matmul(T.pn[:, run], T.f2s[:], T.land[:, run], True, True).then_inc(S.mm_near, 1)
+            n_mm += 1
+    g.vector.wait_ge(S.mm_near, n_mm)
+    for run in _runs(near):
+        g.vector.tensor_copy(T.ys[:, run], T.pn[:, run]).then_inc(S.cp_near, 1)
+    g.scalar.wait_ge(S.cp_near, len(_runs(near)))
+    for run in _runs(near):
+        g.scalar.dma_start(T.y[:, run], T.ys[:, run]).then_inc(S.stored, 16)
+
+    if far:
+        g.tensor.wait_ge(S.arr_far, K_FAR * len(far))
+        for run in _runs(far):
+            g.tensor.matmul(T.pf[:, run], T.f2s[:], T.land[:, run], True, True).then_inc(S.mm_far, 1)
+        g.vector.wait_ge(S.mm_far, len(_runs(far)))
+        for run in _runs(far):
+            g.vector.tensor_copy(T.ys[:, run], T.pf[:, run]).then_inc(S.cp_far, 1)
+        g.sync.wait_ge(S.cp_far, len(_runs(far)))
+        for run in _runs(far):
+            g.sync.dma_start(T.y[:, run], T.ys[:, run]).then_inc(S.stored, 16)
+
+    g.wait_ge(S.sent, len(used))
+    g.wait_ge(S.stored, 16 * (len(_runs(near)) + len(_runs(far))))

@@ -3,22 +3,25 @@ from concourse.mybir import AluOpType
 
 P, TK, N = 128, 32, 4
 W = N * TK
+H = P // 2
 K_FAR = 4
-K_NEAR = 4
+K_NEAR = 8
 
 SCRATCH = {
-    "xs": ("sbuf", [P, W], "bfloat16"),
+    "xs": ("sbuf", [P, 2 * W], "bfloat16"),
+    "f1s": ("sbuf", [P, 2 * P], "bfloat16"),
     "ts": ("sbuf", [P, W], "bfloat16"),
-    "f1s": ("sbuf", [P, P], "bfloat16"),
     "f2s": ("sbuf", [P, P], "bfloat16"),
     "us": ("sbuf", [P, W], "bfloat16"),
     "land": ("sbuf", [P, W], "bfloat16"),
+    "tl": ("sbuf", [P, W], "bfloat16"),
     "ys": ("sbuf", [P, W], "bfloat16"),
-    "pu": ("psum", [P, 512], "float32"),
+    "puf": ("psum", [P, 512], "float32"),
+    "pun": ("psum", [P, 512], "float32"),
     "pn": ("psum", [P, 512], "float32"),
     "pf": ("psum", [P, 512], "float32"),
 }
-SEMAPHORES = ["ld_mm", "ld_t", "ld_f2", "mm_u", "u_ok", "sent", "arr_near", "arr_far",
+SEMAPHORES = ["ld_mm", "ld_t", "ld_f2", "mm_uf", "mm_un", "u_ok", "nr_ok", "sent", "arr_near", "arr_far",
               "mm_near", "mm_far", "cp_near", "cp_far", "stored"]
 
 
@@ -57,51 +60,77 @@ def rank_program(g, core, T, topo):
     far = [j for j in range(len(T.cores)) if j not in near]
     near_peers = [j for j in near if j != r]
 
-    g.sync.dma_start(T.xs[:], T.x[:]).then_inc(S.ld_mm, 16)
-    g.scalar.dma_start(T.f1s[:], T.f1[:]).then_inc(S.ld_mm, 16)
-    g.sync.dma_start(T.ts[:], T.t[:]).then_inc(S.ld_t, 16)
-    g.sync.dma_start(T.f2s[:], T.f2[:]).then_inc(S.ld_f2, 16)
-
-    g.tensor.wait_ge(S.ld_mm, 32)
-    g.tensor.matmul(T.pu[:, 0:W], T.f1s[:], T.xs[:], True, True).then_inc(S.mm_u, 1)
-    g.vector.wait_ge(S.ld_t, 16)
-    g.vector.wait_ge(S.mm_u, 1)
-    g.vector.tensor_tensor(T.us[:], T.pu[:, 0:W], T.ts[:], AluOpType.mult).then_inc(S.u_ok, 1)
-
     used = []
-    plan = []
-    for j in far:
-        free = [e for e in _engines(topo.mask(core, T.cores[j])) if e not in used]
-        plan.append((j, free[:K_FAR], S.arr_far))
-        used += free[:K_FAR]
+    eng = {}
     off_chip = []
     for j in far:
         off_chip += _engines(topo.mask(core, T.cores[j]))
+        free = [e for e in _engines(topo.mask(core, T.cores[j])) if e not in used]
+        eng[j] = free[:K_FAR]
+        used += eng[j]
     for j in near_peers:
         free = [e for e in _engines(topo.mask(core, T.cores[j])) if e not in used]
         pref = [e for e in free if e not in off_chip] or free
-        share = len(pref) // len(near_peers)
-        pick = pref[::max(1, share // K_NEAR)][:K_NEAR]
-        plan.append((j, pick, S.arr_near))
-        used += pick
-    transfers = []
-    for j, es, sem in plan:
-        rid, pid = topo.addr(T.cores[j], core)
-        transfers.append(RemoteDMATransfer(dst_ids=[DstId(rid=rid, pnc=pid)], dma_engine_mask=_to_mask(es),
-                                           remote_sem=sem, src=T.us[:, _blk(j)], dst=T.land[:, _blk(r)]))
-    g.wait_ge(S.u_ok, 1)
-    g.remote_dma_fused(transfers, local_sem=S.sent)
+        eng[j] = pref[:K_NEAR]
+        used += eng[j]
 
-    g.tensor.wait_ge(S.ld_f2, 16)
-    g.tensor.wait_ge(S.u_ok, 1)
-    g.tensor.matmul(T.pn[:, _blk(r)], T.f2s[:], T.us[:, _blk(r)], True, True).then_inc(S.mm_near, 1)
-    n_mm = 1
+    def transfer(j, sem, src, dst):
+        rid, pid = topo.addr(T.cores[j], core)
+        return RemoteDMATransfer(dst_ids=[DstId(rid=rid, pnc=pid)], dma_engine_mask=_to_mask(eng[j]),
+                                 remote_sem=sem, src=src, dst=dst)
+
+    g.sync.dma_start(T.ts[:], T.t[:]).then_inc(S.ld_t, 16)
+    g.scalar.dma_start(T.f1s[0:H, :], T.f1[:]).then_inc(S.ld_mm, 16)
+    g.sync.dma_start(T.xs[0:H, :], T.x[:]).then_inc(S.ld_mm, 16)
+    g.sync.dma_start(T.f2s[:], T.f2[:]).then_inc(S.ld_f2, 16)
+
+    n_sent = 0
     if near_peers:
-        g.tensor.wait_ge(S.arr_near, K_NEAR * len(near_peers))
-        for run in _runs(near_peers):
-            g.tensor.matmul(T.pn[:, run], T.f2s[:], T.land[:, run], True, True).then_inc(S.mm_near, 1)
-            n_mm += 1
-    g.vector.wait_ge(S.mm_near, n_mm)
+        g.wait_ge(S.ld_t, 16)
+        g.remote_dma_fused([transfer(j, S.arr_near, T.ts[:, _blk(j)], T.tl[:, _blk(r)]) for j in near_peers],
+                           local_sem=S.sent)
+        n_sent += sum(len(eng[j]) for j in near_peers)
+
+    def first_mm(bank, run, sem):
+        g.tensor.matmul(bank[:, run], T.f1s[0:H, 0:P], T.xs[0:H, run], True, False)
+        odd = slice(W + run.start, W + run.stop)
+        g.tensor.matmul(bank[:, run], T.f1s[0:H, P:2 * P], T.xs[0:H, odd], False, True).then_inc(sem, 1)
+
+    g.tensor.wait_ge(S.ld_mm, 32)
+    for run in _runs(far):
+        first_mm(T.puf, run, S.mm_uf)
+    for run in _runs(near):
+        first_mm(T.pun, run, S.mm_un)
+
+    n_u = 0
+    g.vector.wait_ge(S.ld_t, 16)
+    if far:
+        g.vector.wait_ge(S.mm_uf, len(_runs(far)))
+        for run in _runs(far):
+            g.vector.tensor_tensor(T.us[:, run], T.puf[:, run], T.ts[:, run], AluOpType.mult).then_inc(S.u_ok, 1)
+            n_u += 1
+    g.vector.wait_ge(S.mm_un, len(_runs(near)))
+    for j in near_peers:
+        g.vector.tensor_copy(T.us[:, _blk(j)], T.pun[:, _blk(j)]).then_inc(S.u_ok, 1)
+        n_u += 1
+    g.vector.tensor_tensor(T.land[:, _blk(r)], T.pun[:, _blk(r)], T.ts[:, _blk(r)], AluOpType.mult).then_inc(S.nr_ok, 1)
+
+    g.wait_ge(S.u_ok, n_u)
+    g.remote_dma_fused([transfer(j, S.arr_far, T.us[:, _blk(j)], T.land[:, _blk(r)]) for j in far]
+                       + [transfer(j, S.arr_near, T.us[:, _blk(j)], T.land[:, _blk(r)]) for j in near_peers],
+                       local_sem=S.sent)
+    n_sent += len(used)
+
+    if near_peers:
+        g.vector.wait_ge(S.arr_near, 2 * K_NEAR * len(near_peers))
+        for j in near_peers:
+            g.vector.tensor_tensor(T.land[:, _blk(j)], T.land[:, _blk(j)], T.tl[:, _blk(j)],
+                                   AluOpType.mult).then_inc(S.nr_ok, 1)
+    g.tensor.wait_ge(S.ld_f2, 16)
+    g.tensor.wait_ge(S.nr_ok, len(near))
+    for run in _runs(near):
+        g.tensor.matmul(T.pn[:, run], T.f2s[:], T.land[:, run], True, True).then_inc(S.mm_near, 1)
+    g.vector.wait_ge(S.mm_near, len(_runs(near)))
     for run in _runs(near):
         g.vector.tensor_copy(T.ys[:, run], T.pn[:, run]).then_inc(S.cp_near, 1)
     g.scalar.wait_ge(S.cp_near, len(_runs(near)))
@@ -119,5 +148,5 @@ def rank_program(g, core, T, topo):
         for run in _runs(far):
             g.sync.dma_start(T.y[:, run], T.ys[:, run]).then_inc(S.stored, 16)
 
-    g.wait_ge(S.sent, len(used))
+    g.wait_ge(S.sent, n_sent)
     g.wait_ge(S.stored, 16 * (len(_runs(near)) + len(_runs(far))))

from concourse.bass import DstId, RemoteDMATransfer
from concourse.mybir import AluOpType

P, TK, N = 128, 32, 4
W = N * TK
H = P // 2
K_FAR = 4
K_NEAR = 8

SCRATCH = {
    "xs": ("sbuf", [P, 2 * W], "bfloat16"),
    "f1s": ("sbuf", [P, 2 * P], "bfloat16"),
    "ts": ("sbuf", [P, W], "bfloat16"),
    "f2s": ("sbuf", [P, P], "bfloat16"),
    "us": ("sbuf", [P, W], "bfloat16"),
    "land": ("sbuf", [P, W], "bfloat16"),
    "tl": ("sbuf", [P, W], "bfloat16"),
    "ys": ("sbuf", [P, W], "bfloat16"),
    "puf": ("psum", [P, 512], "float32"),
    "pun": ("psum", [P, 512], "float32"),
    "pn": ("psum", [P, 512], "float32"),
    "pf": ("psum", [P, 512], "float32"),
}
SEMAPHORES = ["ld_mm", "ld_t", "ld_f2", "mm_uf", "mm_un", "u_ok", "nr_ok", "sent", "arr_near", "arr_far",
              "mm_near", "mm_far", "cp_near", "cp_far", "stored"]


def _blk(j):
    return slice(TK * j, TK * j + TK)


def _runs(js):
    out = []
    for j in sorted(js):
        if out and out[-1][1] == j:
            out[-1][1] = j + 1
        else:
            out.append([j, j + 1])
    return [slice(TK * a, TK * b) for a, b in out]


def _engines(m):
    return [e for e in range(m.bit_length()) if (m >> e) & 1]


def _to_mask(es):
    m = 0
    for e in es:
        m |= 1 << e
    return m


def rank_program(g, core, T, topo):
    r = T.rank_of(core)
    if r is None:
        return
    S = T.sem
    here = (topo.host(core), topo.chip(core))
    near = [j for j, c in enumerate(T.cores) if (topo.host(c), topo.chip(c)) == here]
    far = [j for j in range(len(T.cores)) if j not in near]
    near_peers = [j for j in near if j != r]

    used = []
    eng = {}
    off_chip = []
    for j in far:
        off_chip += _engines(topo.mask(core, T.cores[j]))
        free = [e for e in _engines(topo.mask(core, T.cores[j])) if e not in used]
        eng[j] = free[:K_FAR]
        used += eng[j]
    for j in near_peers:
        free = [e for e in _engines(topo.mask(core, T.cores[j])) if e not in used]
        pref = [e for e in free if e not in off_chip] or free
        eng[j] = pref[:K_NEAR]
        used += eng[j]

    def transfer(j, sem, src, dst):
        rid, pid = topo.addr(T.cores[j], core)
        return RemoteDMATransfer(dst_ids=[DstId(rid=rid, pnc=pid)], dma_engine_mask=_to_mask(eng[j]),
                                 remote_sem=sem, src=src, dst=dst)

    g.sync.dma_start(T.ts[:], T.t[:]).then_inc(S.ld_t, 16)
    g.scalar.dma_start(T.f1s[0:H, :], T.f1[:]).then_inc(S.ld_mm, 16)
    g.sync.dma_start(T.xs[0:H, :], T.x[:]).then_inc(S.ld_mm, 16)
    g.sync.dma_start(T.f2s[:], T.f2[:]).then_inc(S.ld_f2, 16)

    n_sent = 0
    if near_peers:
        g.wait_ge(S.ld_t, 16)
        g.remote_dma_fused([transfer(j, S.arr_near, T.ts[:, _blk(j)], T.tl[:, _blk(r)]) for j in near_peers],
                           local_sem=S.sent)
        n_sent += sum(len(eng[j]) for j in near_peers)

    def first_mm(bank, run, sem):
        g.tensor.matmul(bank[:, run], T.f1s[0:H, 0:P], T.xs[0:H, run], True, False)
        odd = slice(W + run.start, W + run.stop)
        g.tensor.matmul(bank[:, run], T.f1s[0:H, P:2 * P], T.xs[0:H, odd], False, True).then_inc(sem, 1)

    g.tensor.wait_ge(S.ld_mm, 32)
    for run in _runs(far):
        first_mm(T.puf, run, S.mm_uf)
    for run in _runs(near):
        first_mm(T.pun, run, S.mm_un)

    n_u = 0
    g.vector.wait_ge(S.ld_t, 16)
    if far:
        g.vector.wait_ge(S.mm_uf, len(_runs(far)))
        for run in _runs(far):
            g.vector.tensor_tensor(T.us[:, run], T.puf[:, run], T.ts[:, run], AluOpType.mult).then_inc(S.u_ok, 1)
            n_u += 1
    g.vector.wait_ge(S.mm_un, len(_runs(near)))
    for j in near_peers:
        g.vector.tensor_copy(T.us[:, _blk(j)], T.pun[:, _blk(j)]).then_inc(S.u_ok, 1)
        n_u += 1
    g.vector.tensor_tensor(T.land[:, _blk(r)], T.pun[:, _blk(r)], T.ts[:, _blk(r)], AluOpType.mult).then_inc(S.nr_ok, 1)

    g.wait_ge(S.u_ok, n_u)
    g.remote_dma_fused([transfer(j, S.arr_far, T.us[:, _blk(j)], T.land[:, _blk(r)]) for j in far]
                       + [transfer(j, S.arr_near, T.us[:, _blk(j)], T.land[:, _blk(r)]) for j in near_peers],
                       local_sem=S.sent)
    n_sent += len(used)

    if near_peers:
        g.vector.wait_ge(S.arr_near, 2 * K_NEAR * len(near_peers))
        for j in near_peers:
            g.vector.tensor_tensor(T.land[:, _blk(j)], T.land[:, _blk(j)], T.tl[:, _blk(j)],
                                   AluOpType.mult).then_inc(S.nr_ok, 1)
    g.tensor.wait_ge(S.ld_f2, 16)
    g.tensor.wait_ge(S.nr_ok, len(near))
    for run in _runs(near):
        g.tensor.matmul(T.pn[:, run], T.f2s[:], T.land[:, run], True, True).then_inc(S.mm_near, 1)
    g.vector.wait_ge(S.mm_near, len(_runs(near)))
    for run in _runs(near):
        g.vector.tensor_copy(T.ys[:, run], T.pn[:, run]).then_inc(S.cp_near, 1)
    g.scalar.wait_ge(S.cp_near, len(_runs(near)))
    for run in _runs(near):
        g.scalar.dma_start(T.y[:, run], T.ys[:, run]).then_inc(S.stored, 16)

    if far:
        g.tensor.wait_ge(S.arr_far, K_FAR * len(far))
        for run in _runs(far):
            g.tensor.matmul(T.pf[:, run], T.f2s[:], T.land[:, run], True, True).then_inc(S.mm_far, 1)
        g.vector.wait_ge(S.mm_far, len(_runs(far)))
        for run in _runs(far):
            g.vector.tensor_copy(T.ys[:, run], T.pf[:, run]).then_inc(S.cp_far, 1)
        g.sync.wait_ge(S.cp_far, len(_runs(far)))
        for run in _runs(far):
            g.sync.dma_start(T.y[:, run], T.ys[:, run]).then_inc(S.stored, 16)

    g.wait_ge(S.sent, n_sent)
    g.wait_ge(S.stored, 16 * (len(_runs(near)) + len(_runs(far))))
